import numpy as np
import ml_dtypes


def mxq(x, axis, fmt="e4m3"):
    dtype, down = {"e4m3": (ml_dtypes.float8_e4m3fn, 7), "e5m2": (ml_dtypes.float8_e5m2, 14)}[fmt]
    v = np.moveaxis(np.asarray(x, np.float32).astype(ml_dtypes.bfloat16).astype(np.float64), axis, -1)
    blocks = v.reshape(v.shape[:-1] + (-1, 32))
    amax = np.abs(blocks).max(-1, keepdims=True)
    byte = np.maximum(np.where(amax > 0, np.frexp(amax)[1] - 1 + 127, 0) - down, 1)
    scale = np.exp2(byte - 127.0)
    codes = (blocks / scale).astype(np.float32).astype(dtype).astype(np.float64)
    return np.moveaxis((codes * scale).reshape(v.shape), -1, axis)


WIDE = False


def mx_kscale(k):
    if not WIDE:
        return np.ones(k)
    levels = np.array([30, -30])
    if k % 512:
        return np.exp2(np.random.permutation(np.resize(levels, k // 32))).repeat(32)
    a = np.empty((k // 512, 16))
    for p in range(k // 512):
        a[p, :8] = np.random.permutation(np.resize(levels, 8))
        for g in range(8):
            far = levels[np.abs(levels - a[p, g]) >= 10]
            a[p, g + 8] = far[np.random.randint(len(far))]
    return np.exp2(a.ravel()).repeat(32)


def f64(x):
    return np.asarray(x).astype(np.float64)


def striped(idx):
    return np.tile(np.asarray(idx).reshape(-1, 16).T, (8, 1)).astype(np.uint16)


def unstriped(offs):
    return offs[:16].T.reshape(-1).astype(np.int64)


def striped8(idx):
    return np.asarray(idx).reshape(8, -1, 16).transpose(0, 2, 1).reshape(128, -1).astype(np.uint16)


def unstriped8(offs):
    return offs.reshape(8, 16, -1).transpose(0, 2, 1).reshape(8, -1).astype(np.int64)


def pick8(x, idx, run):
    r = np.arange(len(x))
    return x[r[:, None], idx[r % (8 * run) // run]]


E2M1 = np.array([0.0, 0.5, 1.0, 1.5, 2.0, 3.0, 4.0, 6.0, -0.0, -0.5, -1.0, -1.5, -2.0, -3.0, -4.0, -6.0])


def pack_weight(w, fmt):
    k, n = w.shape
    w = f64(np.asarray(w, np.float32).astype(ml_dtypes.bfloat16)).reshape(k // 32, 32, n)
    amax = np.abs(w).max(1)
    if fmt in ("e4m3", "e5m2"):
        byte = np.frexp(amax)[1] - 1 + 127 - (7 if fmt == "e4m3" else 14)
    else:
        mant, ex = np.frexp(amax / 6.0)
        byte = np.where(mant > 0.5, ex, ex - 1) + 127
    byte = np.clip(np.where(amax > 0, byte, 1), 1, 254)
    scaled = (w * np.exp2(127.0 - byte)[:, None, :]).reshape(k, n).astype(np.float32)
    by_word = np.ascontiguousarray(scaled.reshape(k // 512, 128, 4, n).transpose(0, 1, 3, 2))
    if fmt in ("e4m3", "e5m2"):
        words = by_word.astype(ml_dtypes.float8_e4m3fn if fmt == "e4m3" else ml_dtypes.float8_e5m2).view(np.uint8)
    else:
        c = by_word.astype(ml_dtypes.float4_e2m1fn).view(np.uint8) & 0xF
        words = (c[..., 0::2] | (c[..., 1::2] << 4)).reshape(k // 512, 128, 2 * n)
    return np.ascontiguousarray(words), np.ascontiguousarray(byte.astype(np.uint8).reshape(k // 512, 16, n))


def unpack_weight(words, scales, fmt):
    g, _, n = scales.shape
    words = np.ascontiguousarray(words).reshape(g, 128, n, -1)
    if fmt in ("e4m3", "e5m2"):
        vals = words.view(ml_dtypes.float8_e4m3fn if fmt == "e4m3" else ml_dtypes.float8_e5m2).astype(np.float64)
    else:
        nib = np.empty((g, 128, n, 4), np.uint8)
        nib[..., 0::2] = words & 0xF
        nib[..., 1::2] = words >> 4
        vals = E2M1[nib]
    vals = vals * np.repeat(np.exp2(scales.astype(np.float64) - 127.0), 8, axis=1)[..., None]
    return vals.transpose(0, 1, 3, 2).reshape(g * 512, n)


def e4m3fn_bytes(y):
    return np.clip(np.asarray(y, np.float64), -448.0, 448.0).astype(np.float32).astype(ml_dtypes.float8_e4m3fn).view(np.uint8)


def e4m3fn_values(b):
    return np.asarray(b, np.uint8).view(ml_dtypes.float8_e4m3fn).astype(np.float64)


K, T, J, R, C, V, O, N = 512, 1024, 256, 512, 512, 1024, 256, 256


def setup_inputs():
    n = np.random.standard_normal
    idx = np.random.permutation(T)[:J]
    idx2 = np.random.permutation(V)[:J]
    idx3 = np.stack([np.random.permutation(C)[:J] for _ in range(8)])
    idx4 = np.stack([np.random.permutation(C)[:O] for _ in range(8)])
    fk = mx_kscale(K)
    fr = mx_kscale(R)
    xtp = pack_weight(n((K, T)) / fk[:, None], "e2m1")
    wp = pack_weight(n((K, R)) * 1 / np.sqrt(K) * fk[:, None], "e5m2")
    wbp = pack_weight(n((R, N)) * 1 / np.sqrt(R) / fr[:, None], "e4m3")
    return {
        "xt_words": xtp[0],
        "xt_scales": xtp[1],
        "w_words": wp[0],
        "w_scales": wp[1],
        "ca": e4m3fn_bytes(60.0 * n((R, V))),
        "st": (np.random.uniform(0.004, 0.012, (R, 1)) * fr[:, None]).astype(np.float32),
        "wb_words": wbp[0],
        "wb_scales": wbp[1],
        "offs": striped(idx),
        "offs2": striped(idx2),
        "offs3": striped8(idx3),
        "offs4": striped8(idx4),
    }


def reference(xt_words, xt_scales, w_words, w_scales, ca, st, wb_words, wb_scales, offs, offs2, offs3, offs4):
    idx = unstriped(offs)
    idx2 = unstriped(offs2)
    idx3 = unstriped8(offs3)
    idx4 = unstriped8(offs4)
    xtu = unpack_weight(xt_words, xt_scales, "e2m1")
    wu = unpack_weight(w_words, w_scales, "e5m2")
    wbu = unpack_weight(wb_words, wb_scales, "e4m3")
    xtidxg = xtu[:, idx]
    a = wu.T @ xtidxg
    g1 = e4m3fn_values(ca)[:, idx2] * f64(st)
    h1 = a * g1
    pw = np.zeros((R, C))
    pw[np.arange(R)[:, None], idx3[np.arange(R) % 512 // 64]] = h1
    hid = pick8(pw, idx4, 64)
    hidq = mxq(hid, 0, "e5m2")
    p = wbu.T @ hidq
    return p

from contextlib import ExitStack

import concourse.mybir as mybir

K, T, J, R, C, V, O, N = 512, 1024, 256, 512, 512, 1024, 256, 256
FLOPS = 2 * K * R * J + 2 * R * N * O

F32 = mybir.dt.float32
BF16 = mybir.dt.bfloat16
I32 = mybir.dt.int32
U32 = mybir.dt.uint32
U16 = mybir.dt.uint16
U8 = mybir.dt.uint8
FP8 = mybir.dt.float8_e4m3fn
E4M3X4 = mybir.dt.float8_e4m3fn_x4
E5M2X4 = mybir.dt.float8_e5m2_x4
E2M1X4 = mybir.dt.float4_e2m1fn_x4
MULT = mybir.AluOpType.mult
COPY = mybir.ActivationFunctionType.Copy

P = 128
PACK = 4
QUAD = 32
HALF = O // 2


def tile_list_groupboards_kernel(
    tc, xt_words, xt_scales, w_words, w_scales, ca, st, wb_words, wb_scales, offs, offs2, offs3, offs4, out
):
    nc = tc.nc
    with ExitStack() as ctx:
        sb = ctx.enter_context(tc.tile_pool(name="sb", bufs=1))
        ps = ctx.enter_context(tc.psum_pool(name="ps", bufs=1))

        def tile(name, shape, dtype):
            return sb.tile(shape, dtype, name=name, align_bytes=64)

        tok_list = tile("tok_list", [P, J // 16], U16)
        gate_list = tile("gate_list", [P, J // 16], U16)
        put_list = tile("put_list", [P, J // 16], U16)
        take_list = tile("take_list", [P, O // 16], U16)

        x_words = tile("x_words", [P, T], U16)
        x_scales = tile("x_scales", [P, T], U8)
        w_raw = tile("w_raw", [P, R], I32)
        ws_raw = tile("ws_raw", [P, R], U8)
        w_dealt = tile("w_dealt", [P, PACK, P], I32)
        ws_dealt = tile("ws_dealt", [P, PACK, P], U8)
        steps = tile("steps", [P, PACK], F32)
        wb_sb = tile("wb_sb", [P, N], I32)
        wbs_sb = tile("wbs_sb", [P, N], U8)
        gates = [tile(f"gates{t}", [P, V], U8) for t in range(PACK)]
        boards = [tile(f"board{t}", [P, C], F32) for t in range(PACK)]

        def load_scale_rows(plane, rows):
            for q in range(PACK):
                nc.sync.dma_start(
                    plane[QUAD * q : QUAD * (q + 1), :].bitcast(I32),
                    rows[0, PACK * q : PACK * (q + 1), :].bitcast(I32).partition_broadcast(QUAD // PACK),
                )

        nc.gpsimd.dma_start(w_raw[:], w_words[0].rearrange("p c b -> p (c b)").bitcast(I32))
        nc.gpsimd.dma_start(steps[:], st.rearrange("(p t) u -> p (t u)", t=PACK))
        for t in range(PACK):
            nc.vector.memset(boards[t][:], 0.0)

        ca_rows = ca.rearrange("(p t) v -> t p v", t=PACK)
        nc.sync.dma_start(tok_list[:], offs)
        nc.sync.dma_start(gate_list[:], offs2)
        load_scale_rows(x_scales, xt_scales)
        nc.sync.dma_start(x_words[:].bitcast(I32), xt_words[0].bitcast(I32))
        nc.sync.dma_start(gates[0][:], ca_rows[0])
        load_scale_rows(ws_raw, w_scales)
        nc.sync.dma_start(put_list[:], offs3)
        for t in range(1, PACK):
            nc.sync.dma_start(gates[t][:], ca_rows[t])
        nc.sync.dma_start(take_list[:], offs4)
        nc.sync.dma_start(wb_sb[:], wb_words[0].rearrange("p c b -> p (c b)").bitcast(I32))
        load_scale_rows(wbs_sb, wb_scales)

        def entries(lst, lo, hi):
            return lst[:, lo // 16 : hi // 16]

        xg_words = tile("xg_words", [P, J], U16)
        xg_scales = tile("xg_scales", [P, J], U8)
        nc.scalar.copy(
            w_dealt[:].bitcast(U32).rearrange("p t m -> p m t"),
            w_raw[:].bitcast(U32).rearrange("p (m t) -> p m t", t=PACK),
        )
        nc.vector.tensor_copy(xg_scales[:], x_scales[:].indirect(tok_list[:]))
        nc.vector.tensor_copy(xg_words[:], x_words[:].indirect(tok_list[:]))

        codes = [tile(f"codes{t}", [P, J], U8) for t in range(PACK)]
        g1 = [tile(f"g1_{t}", [P, J], F32) for t in range(PACK)]
        h1 = [tile(f"h1_{t}", [P, J], F32) for t in range(PACK)]
        ws_by_t = ws_raw[:].rearrange("p (m t) -> p t m", t=PACK)

        def look_up(t):
            nc.vector.tensor_copy(codes[t][:], gates[t][:].indirect(gate_list[:]))

        def gate(t):
            nc.vector.tensor_scalar(g1[t][:], codes[t][:].bitcast(FP8), steps[:, t : t + 1], None, MULT)

        def put(t):
            a_ps = ps.tile([P, J], F32, name=f"a_ps{t}", tag=f"bank{t}")
            nc.tensor.matmul_mx(
                out=a_ps[:],
                lhsT=w_dealt[:, t, :].bitcast(E5M2X4),
                lhsT_scale=ws_dealt[:, t, :],
                rhs=xg_words[:].bitcast(E2M1X4),
                rhs_scale=xg_scales[:],
                start=True,
                stop=True,
            )
            nc.vector.tensor_tensor(h1[t][:], a_ps[:], g1[t][:], MULT)
            nc.scalar.activation(boards[t][:].indirect(put_list[:]), h1[t][:], COPY)

        look_up(0)
        nc.vector.tensor_copy(ws_dealt[:, 0, :], ws_by_t[:, 0, :])
        gate(0)
        nc.vector.tensor_copy(
            ws_dealt[:, 1:, :].rearrange("p t m -> p m t"), ws_by_t[:, 1:, :].rearrange("p t m -> p m t")
        )
        put(0)
        look_up(1)
        for t in range(1, PACK):
            if t + 1 < PACK:
                look_up(t + 1)
            gate(t)
            put(t)

        hid = tile("hid", [P, PACK, O], BF16)
        woven = tile("woven", [P, O, PACK], BF16)
        last = PACK - 1
        for t in range(last):
            nc.vector.tensor_copy(hid[:, t, :], boards[t][:].indirect(take_list[:]))
        nc.vector.tensor_copy(woven[:, :, :last], hid[:, :last, :].rearrange("p t o -> p o t"))
        nc.vector.tensor_copy(hid[:, last, :HALF], boards[last][:].indirect(entries(take_list, 0, HALF)))
        nc.scalar.activation(hid[:, last, HALF:], boards[last][:].indirect(entries(take_list, HALF, O)), COPY)

        halves = [slice(u * HALF, (u + 1) * HALF) for u in range(2)]
        for u in range(2):
            nc.vector.tensor_copy(woven[:, halves[u], last], hid[:, last, halves[u]])
        hq = [tile(f"hq{u}", [P, HALF], U32) for u in range(2)]
        hs = [tile(f"hs{u}", [P, HALF], U8) for u in range(2)]
        for u in range(2):
            nc.vector.quantize_mx(
                out=hq[u][:].bitcast(E5M2X4),
                scales=hs[u][:],
                in_=woven[:, halves[u], :].rearrange("p o t -> p (o t)"),
            )
        for u in range(2):
            for m in range(N // P):
                o_ps = ps.tile([P, HALF], F32, name=f"o_ps{u}{m}", tag=f"bank{2 * u + m}")
                nc.tensor.matmul_mx(
                    out=o_ps[:],
                    lhsT=wb_sb[:, m * P : (m + 1) * P].bitcast(E4M3X4),
                    lhsT_scale=wbs_sb[:, m * P : (m + 1) * P],
                    rhs=hq[u][:].bitcast(E5M2X4),
                    rhs_scale=hs[u][:],
                    start=True,
                    stop=True,
                )
                res = tile(f"res{u}{m}", [P, HALF], F32)
                dest = out[m * P : (m + 1) * P, halves[u]]
                if m == 0:
                    nc.scalar.copy(res[:], o_ps[:])
                    nc.scalar.dma_start(dest, res[:])
                else:
                    nc.vector.tensor_copy(res[:], o_ps[:])
                    nc.sync.dma_start(dest, res[:])
